import numpy as np
import ml_dtypes


def mxq(x, axis, fmt="e4m3"):
    dtype, down = {"e4m3": (ml_dtypes.float8_e4m3fn, 7), "e5m2": (ml_dtypes.float8_e5m2, 14)}[fmt]
    v = np.moveaxis(np.asarray(x, np.float32).astype(ml_dtypes.bfloat16).astype(np.float64), axis, -1)
    blocks = v.reshape(v.shape[:-1] + (-1, 32))
    amax = np.abs(blocks).max(-1, keepdims=True)
    byte = np.maximum(np.where(amax > 0, np.frexp(amax)[1] - 1 + 127, 0) - down, 1)
    scale = np.exp2(byte - 127.0)
    codes = (blocks / scale).astype(np.float32).astype(dtype).astype(np.float64)
    return np.moveaxis((codes * scale).reshape(v.shape), -1, axis)


WIDE = False


def mx_kscale(k):
    if not WIDE:
        return np.ones(k)
    levels = np.array([10, -10, 5, -5, 0])
    if k % 512:
        return np.exp2(np.random.permutation(np.resize(levels, k // 32))).repeat(32)
    a = np.empty((k // 512, 16))
    for p in range(k // 512):
        a[p, :8] = np.random.permutation(np.resize(levels, 8))
        for g in range(8):
            far = levels[np.abs(levels - a[p, g]) >= 10]
            a[p, g + 8] = far[np.random.randint(len(far))]
    return np.exp2(a.ravel()).repeat(32)


def f64(x):
    return np.asarray(x).astype(np.float64)


def striped(idx):
    return np.tile(idx.reshape(-1, 16).T, (8, 1)).astype(np.uint16)


def unstriped(offs):
    return offs[:16].T.reshape(-1).astype(np.int64)


def striped8(idx):
    return np.concatenate([x.reshape(-1, 16).T for x in idx]).astype(np.uint16)


def runs(offs, k):
    lists = np.stack([offs[16 * r : 16 * r + 16].T.reshape(-1) for r in range(8)]).astype(np.int64)
    return lists[np.arange(k) % 512 // 64]


def pack_weight(w):
    k, n = w.shape
    w = f64(np.asarray(w, np.float32).astype(ml_dtypes.bfloat16)).reshape(k // 32, 32, n)
    amax = np.abs(w).max(1)
    byte = np.clip(np.where(amax > 0, np.frexp(amax)[1] - 1 + 127 - 7, 1), 1, 254)
    scaled = (w * np.exp2(127.0 - byte)[:, None, :]).reshape(k, n).astype(np.float32)
    words = np.ascontiguousarray(scaled.reshape(k // 512, 128, 4, n).transpose(0, 1, 3, 2)).astype(ml_dtypes.float8_e4m3fn).view(np.uint8)
    return words, np.ascontiguousarray(byte.astype(np.uint8).reshape(k // 512, 16, n))


def unpack_weight(words, scales):
    g, p, n, _ = words.shape
    vals = np.ascontiguousarray(words).view(ml_dtypes.float8_e4m3fn).astype(np.float64) * np.repeat(np.exp2(scales.astype(np.float64) - 127.0), 8, axis=1)[..., None]
    return vals.transpose(0, 1, 3, 2).reshape(g * 512, n)


def relu(v):
    return np.maximum(v, 0.0)


K, T, S, H, C = 512, 2048, 512, 512, 512


def setup_inputs():
    n = np.random.standard_normal
    s = mx_kscale(K)[:, None]
    packed_xT = pack_weight(n((K, T)) * s)
    return {
        "x_words": packed_xT[0],
        "x_scales": packed_xT[1],
        "w1": (n((K, H)) / np.sqrt(K) / s).astype(np.float32),
        "gs": (np.random.uniform(0.5, 1.5, (K, 1)) / s).astype(np.float32),
        "gs2": (np.random.uniform(0.5, 1.5, (K, 1)) / s).astype(np.float32),
        "offs": striped(np.random.permutation(T)[:S]),
        "n1": striped8(np.stack([np.random.permutation(S) for _ in range(8)])),
        "n2": striped8(np.stack([np.random.permutation(S) for _ in range(8)])),
        "n3": striped(np.random.permutation(S)),
        "ca": striped(np.random.permutation(T)[:C]),
        "cb": striped(np.random.permutation(T)[:C]),
        "n4": striped(np.random.permutation(S)),
        "n5": striped(np.random.permutation(S)),
    }


def reference(x_words, x_scales, w1, gs, gs2, offs, n1, n2, n3, ca, cb, n4, n5):
    x_ca = unpack_weight(x_words, x_scales)[:, unstriped(ca)]
    xq = unpack_weight(x_words, x_scales)[:, unstriped(offs)]
    y = mxq(f64(w1), 0, "e4m3").T @ xq
    sq = (y) ** 2
    z = f64(gs) * ((y[np.arange(H)[:, None], runs(n2, H)]) / (np.sqrt(sq + sq[np.arange(H)[:, None], runs(n1, H)] + 0.25)))
    a = 0.0625 * ((x_ca.T @ mxq(z, 0, "e4m3")))
    x_cb = unpack_weight(x_words, x_scales)[:, unstriped(cb)]
    rl = relu(y)
    ds = np.zeros((H, S))
    ds[:, unstriped(n3)] = rl
    z2 = f64(gs2) * (ds - (0.5 * y))
    b = 0.0625 * ((x_cb.T @ mxq(z2, 0, "e4m3")))
    return a[:, unstriped(n4)] - (np.tanh(b) * b[:, unstriped(n5)])

@@ -1,0 +1,216 @@
+from contextlib import ExitStack
+
+import concourse.mybir as mybir
+
+K, T, S, H, C = 512, 2048, 512, 512, 512
+FLOPS = 3 * 2 * 512 * 512 * 512
+
+F32 = mybir.dt.float32
+BF16 = mybir.dt.bfloat16
+I32 = mybir.dt.int32
+U32 = mybir.dt.uint32
+U16 = mybir.dt.uint16
+U8 = mybir.dt.uint8
+FP8X4 = mybir.dt.float8_e4m3fn_x4
+ACT = mybir.ActivationFunctionType
+ALU = mybir.AluOpType
+
+P = 128
+PACK = 4
+SPARE = 16
+HALF = S // 2
+
+
+def tile_picked_twocdsoftbrmssend_none_p_kernel(
+    tc, x_words, x_scales, w1, gs, gs2, offs, n1, n2, n3, ca, cb, n4, n5, out
+):
+    nc = tc.nc
+    with ExitStack() as ctx:
+        keep = ctx.enter_context(tc.tile_pool(name="keep", bufs=1))
+        psum = ctx.enter_context(tc.psum_pool(name="psum", bufs=1))
+
+        def sbuf(name, shape, dtype, tag=None):
+            return keep.tile(shape, dtype, name=name, tag=tag or name, align_bytes=64)
+
+        def load_list(name, src):
+            tile = keep.tile([P, S // 16], U16, name=name)
+            nc.sync.dma_start(tile[:], src)
+            return tile
+
+        table_words = sbuf("table_words", [P, T], U32)
+        table_bytes = sbuf("table_bytes", [P, T], U8)
+        nc.vector.memset(table_bytes[:].bitcast(I32), 0)
+
+        w_raw = [sbuf("w_raw%d" % u, [P, PACK, H // 2], F32) for u in range(2)]
+        w_rows = w1.rearrange("(p j) c -> p j c", j=PACK)
+        nc.scalar.dma_start(table_words[:].bitcast(I32), x_words[0].rearrange("p n t -> p (n t)").bitcast(I32))
+        nc.scalar.dma_start(w_raw[0][:], w_rows[:, :, 0 : H // 2])
+        nc.scalar.dma_start(w_raw[1][:], w_rows[:, :, H // 2 : H])
+
+        l_offs = load_list("l_offs", offs)
+        landed_bytes = sbuf("landed_bytes", [P, T // 4], I32)
+        for q in range(4):
+            nc.sync.dma_start(landed_bytes[32 * q : 32 * q + 4, :], x_scales[0, 4 * q : 4 * q + 4, :].bitcast(I32))
+        l_ca = load_list("l_ca", ca)
+        l_cb = load_list("l_cb", cb)
+        l_n3 = load_list("l_n3", n3)
+        l_n1 = load_list("l_n1", n1)
+        l_n2 = load_list("l_n2", n2)
+        l_n5 = load_list("l_n5", n5)
+        l_n4 = load_list("l_n4", n4)
+
+        gain = sbuf("gain", [P, PACK], F32)
+        gain2 = sbuf("gain2", [P, PACK], F32)
+        nc.gpsimd.dma_start(gain2[:], gs2.rearrange("(p t) o -> p (t o)", t=PACK))
+        nc.gpsimd.dma_start(gain[:], gs.rearrange("(p t) o -> p (t o)", t=PACK))
+        quarter = sbuf("quarter", [P, 1], F32)
+        nc.gpsimd.memset(quarter[:], 0.25)
+        a_win = [sbuf("a_win%d" % c, [P, S + SPARE], F32) for c in range(4)]
+        b_win = [sbuf("b_win%d" % c, [P, S + SPARE], F32) for c in range(4)]
+        for tile in a_win + b_win:
+            nc.gpsimd.memset(tile[:, S:], 0.0)
+        minus_half_gain2 = sbuf("minus_half_gain2", [P, PACK], F32)
+        nc.gpsimd.tensor_scalar(minus_half_gain2[:], gain2[:], -0.5, 0.0, ALU.mult, ALU.add)
+
+        def pick_bytes(name, offsets, tag=None):
+            tile = sbuf(name, [P, S], U8, tag)
+            nc.vector.tensor_copy(tile[:], table_bytes[:].indirect(offsets[:]))
+            return tile
+
+        def pick_words(name, offsets, tag=None):
+            tile = sbuf(name, [P, S], U32, tag)
+            nc.vector.tensor_copy(tile[:], table_words[:].indirect(offsets[:]))
+            return tile
+
+        w_bf = sbuf("w_bf", [P, PACK, P, PACK], BF16)
+
+        def cast_w(u):
+            nc.scalar.copy(
+                w_bf[:, :, 64 * u : 64 * u + 64, :].rearrange("p t m j -> p m j t"),
+                w_raw[u][:].rearrange("p j (m t) -> p m j t", t=PACK),
+            )
+
+        for q in range(4):
+            nc.vector.tensor_copy(table_bytes[32 * q : 32 * q + 4, :].bitcast(I32), landed_bytes[32 * q : 32 * q + 4, :])
+        x_bytes = pick_bytes("x_bytes", l_offs)
+        cast_w(0)
+        x_codes = pick_words("x_codes", l_offs)
+        cast_w(1)
+        ca_bytes = pick_bytes("ca_bytes", l_ca)
+        w_codes = [sbuf("w_codes%d" % t, [P, P], U32) for t in range(PACK)]
+        w_bytes = [sbuf("w_bytes%d" % t, [P, P], U8) for t in range(PACK)]
+        y_bank = []
+        for t in range(PACK):
+            nc.vector.quantize_mx(
+                out=w_codes[t][:].bitcast(FP8X4), scales=w_bytes[t][:], in_=w_bf[:, t].rearrange("p m j -> p (m j)")
+            )
+            bank = psum.tile([P, S], F32, name="y_bank%d" % t, tag="bank%d" % t)
+            nc.tensor.matmul_mx(
+                out=bank[:], lhsT=w_codes[t][:].bitcast(FP8X4), lhsT_scale=w_bytes[t][:],
+                rhs=x_codes[:].bitcast(FP8X4), rhs_scale=x_bytes[:], start=True, stop=True,
+            )
+            y_bank.append(bank)
+
+        sq_win = [sbuf("sq_win%d" % t, [P, 2 * S], F32) for t in range(PACK)]
+        y_win = [sbuf("y_win%d" % t, [P, 2 * S], F32) for t in range(PACK)]
+        sent = [sbuf("sent%d" % t, [P, S], F32) for t in range(PACK)]
+        denom = [sbuf("denom%d" % t, [P, S], F32) for t in range(PACK)]
+        inv_root = [sbuf("inv_root%d" % t, [P, S], F32) for t in range(PACK)]
+        z = sbuf("z", [P, PACK, S], F32)
+        z2 = sbuf("z2", [P, PACK, S], F32)
+
+        def square(t):
+            nc.scalar.activation(sq_win[t][:, :S], y_bank[t][:], ACT.Square)
+            nc.sync.dma_start(y_win[t][:, S:], sq_win[t][:, :S])
+
+        def positive_part(t):
+            nc.vector.tensor_scalar(sq_win[t][:, S:], y_bank[t][:], 0.0, gain2[:, t : t + 1], ALU.max, ALU.mult)
+
+        def scaled_y(t):
+            nc.scalar.activation(y_win[t][:, :S], y_bank[t][:], ACT.Copy, scale=gain[:, t : t + 1])
+
+        def send(t, half, on_vector=False):
+            window = sent[t][:].indirect(l_n3[:, 16 * half : 16 * half + 16])
+            src = sq_win[t][:, S + HALF * half : S + HALF * (half + 1)]
+            if on_vector:
+                nc.vector.tensor_copy(window, src)
+            else:
+                nc.scalar.activation(window, src, ACT.Copy)
+
+        def sum_squares(t):
+            nc.vector.tensor_tensor(denom[t][:], sq_win[t][:].indirect(l_n1[:]), y_win[t][:, S:], ALU.add)
+
+        def root(t):
+            nc.scalar.activation(inv_root[t][:], denom[t][:], ACT.Abs_reciprocal_sqrt, bias=quarter[:])
+
+        def make_z(t):
+            nc.vector.tensor_tensor(z[:, t, :], y_win[t][:].indirect(l_n2[:]), inv_root[t][:], ALU.mult)
+
+        def make_z2(t):
+            nc.vector.scalar_tensor_tensor(
+                z2[:, t, :], y_bank[t][:], minus_half_gain2[:, t : t + 1], sent[t][:], ALU.mult, ALU.add
+            )
+
+        def weave(name, planes):
+            tile = sbuf(name, [P, S, PACK], BF16)
+            nc.vector.tensor_copy(
+                tile[:].rearrange("p (c i) t -> p c t i", i=4), planes[:].rearrange("p t (c i) -> p c t i", i=4)
+            )
+            return tile
+
+        def quantise(name, woven):
+            codes = sbuf(name + "_codes", [P, S], U32)
+            scale_bytes = sbuf(name + "_bytes", [P, S], U8)
+            nc.vector.quantize_mx(
+                out=codes[:].bitcast(FP8X4), scales=scale_bytes[:], in_=woven[:].rearrange("p n t -> p (n t)")
+            )
+            return codes, scale_bytes
+
+        def score(name, first_bank, picked_codes, picked_bytes, codes, scale_bytes):
+            banks = []
+            for c in range(4):
+                bank = psum.tile([P, S], F32, name="%s%d" % (name, c), tag="bank%d" % (first_bank + c))
+                cols = slice(P * c, P * (c + 1))
+                nc.tensor.matmul_mx(
+                    out=bank[:], lhsT=picked_codes[:, cols].bitcast(FP8X4), lhsT_scale=picked_bytes[:, cols],
+                    rhs=codes[:].bitcast(FP8X4), rhs_scale=scale_bytes[:], start=True, stop=True,
+                )
+                banks.append(bank)
+            return banks
+
+        for t in range(PACK):
+            square(t)
+            positive_part(t)
+        send(0, 0)
+        for t in range(1, PACK):
+            send(t, 0)
+            send(t, 1)
+        ca_codes = pick_words("ca_codes", l_ca, "w_bf")
+        cb_bytes = pick_bytes("cb_bytes", l_cb, "w_bytes0")
+        cb_codes = pick_words("cb_codes", l_cb, "w_codes0")
+        for t in range(PACK):
+            sum_squares(t)
+        send(0, 1, on_vector=True)
+        for t in range(PACK):
+            make_z2(t)
+        z2_bf = weave("z2_bf", z2)
+        z2_codes, z2_bytes = quantise("z2", z2_bf)
+        b_bank = score("b_bank", 4, cb_codes, cb_bytes, z2_codes, z2_bytes)
+        for t in range(PACK):
+            scaled_y(t)
+            root(t)
+            make_z(t)
+        z_bf = weave("z_bf", z)
+        z_codes, z_bytes = quantise("z", z_bf)
+        a_bank = score("a_bank", 0, ca_codes, ca_bytes, z_codes, z_bytes)
+
+        for c in range(4):
+            minus_tanh = sbuf("minus_tanh%d" % c, [P, S], F32)
+            nc.scalar.activation(minus_tanh[:], b_bank[c][:], ACT.Tanh, scale=-0.0625)
+            nc.scalar.activation(b_win[c][:, :S], b_bank[c][:], ACT.Copy, scale=0.0625)
+            nc.scalar.activation(a_win[c][:, :S], a_bank[c][:], ACT.Copy, scale=0.0625)
+            product = sbuf("product%d" % c, [P, S], F32)
+            nc.vector.tensor_tensor(product[:], b_win[c][:].indirect(l_n5[:]), minus_tanh[:], ALU.mult)
+            result = sbuf("result%d" % c, [P, S], F32)
+            nc.vector.tensor_tensor(result[:], a_win[c][:].indirect(l_n4[:]), product[:], ALU.add)
+            nc.sync.dma_start(out[P * c : P * (c + 1), :], result[:])

@@ -39,7 +39,11 @@ def tile_picked_twocdsoftbrmssend_none_p_kernel(
 
         table_words = sbuf("table_words", [P, T], U32)
         table_bytes = sbuf("table_bytes", [P, T], U8)
-        nc.vector.memset(table_bytes[:].bitcast(I32), 0)
+        nc.gpsimd.memset(table_bytes[:].bitcast(I32), 0)
+        for q in range(4):
+            nc.gpsimd.dma_start(
+                table_bytes[32 * q : 32 * q + 4, :].bitcast(I32), x_scales[0, 4 * q : 4 * q + 4, :].bitcast(I32)
+            )
 
         w_raw = [sbuf("w_raw%d" % u, [P, PACK, H // 2], F32) for u in range(2)]
         w_rows = w1.rearrange("(p j) c -> p j c", j=PACK)
@@ -47,30 +51,27 @@ def tile_picked_twocdsoftbrmssend_none_p_kernel(
         nc.scalar.dma_start(w_raw[0][:], w_rows[:, :, 0 : H // 2])
         nc.scalar.dma_start(w_raw[1][:], w_rows[:, :, H // 2 : H])
 
+        gain = sbuf("gain", [P, PACK], F32)
+        gain2 = sbuf("gain2", [P, PACK], F32)
         l_offs = load_list("l_offs", offs)
-        landed_bytes = sbuf("landed_bytes", [P, T // 4], I32)
-        for q in range(4):
-            nc.sync.dma_start(landed_bytes[32 * q : 32 * q + 4, :], x_scales[0, 4 * q : 4 * q + 4, :].bitcast(I32))
         l_ca = load_list("l_ca", ca)
         l_cb = load_list("l_cb", cb)
+        nc.sync.dma_start(gain2[:], gs2.rearrange("(p t) o -> p (t o)", t=PACK))
         l_n3 = load_list("l_n3", n3)
         l_n1 = load_list("l_n1", n1)
+        nc.sync.dma_start(gain[:], gs.rearrange("(p t) o -> p (t o)", t=PACK))
         l_n2 = load_list("l_n2", n2)
         l_n5 = load_list("l_n5", n5)
         l_n4 = load_list("l_n4", n4)
 
-        gain = sbuf("gain", [P, PACK], F32)
-        gain2 = sbuf("gain2", [P, PACK], F32)
-        nc.gpsimd.dma_start(gain2[:], gs2.rearrange("(p t) o -> p (t o)", t=PACK))
-        nc.gpsimd.dma_start(gain[:], gs.rearrange("(p t) o -> p (t o)", t=PACK))
         quarter = sbuf("quarter", [P, 1], F32)
-        nc.gpsimd.memset(quarter[:], 0.25)
+        nc.vector.memset(quarter[:], 0.25)
         a_win = [sbuf("a_win%d" % c, [P, S + SPARE], F32) for c in range(4)]
         b_win = [sbuf("b_win%d" % c, [P, S + SPARE], F32) for c in range(4)]
         for tile in a_win + b_win:
-            nc.gpsimd.memset(tile[:, S:], 0.0)
+            nc.vector.memset(tile[:, S:], 0.0)
         minus_half_gain2 = sbuf("minus_half_gain2", [P, PACK], F32)
-        nc.gpsimd.tensor_scalar(minus_half_gain2[:], gain2[:], -0.5, 0.0, ALU.mult, ALU.add)
+        nc.vector.tensor_scalar(minus_half_gain2[:], gain2[:], -0.5, None, ALU.mult)
 
         def pick_bytes(name, offsets, tag=None):
             tile = sbuf(name, [P, S], U8, tag)
@@ -90,13 +91,10 @@ def tile_picked_twocdsoftbrmssend_none_p_kernel(
                 w_raw[u][:].rearrange("p j (m t) -> p m j t", t=PACK),
             )
 
-        for q in range(4):
-            nc.vector.tensor_copy(table_bytes[32 * q : 32 * q + 4, :].bitcast(I32), landed_bytes[32 * q : 32 * q + 4, :])
+        x_codes = pick_words("x_codes", l_offs)
         x_bytes = pick_bytes("x_bytes", l_offs)
         cast_w(0)
-        x_codes = pick_words("x_codes", l_offs)
         cast_w(1)
-        ca_bytes = pick_bytes("ca_bytes", l_ca)
         w_codes = [sbuf("w_codes%d" % t, [P, P], U32) for t in range(PACK)]
         w_bytes = [sbuf("w_bytes%d" % t, [P, P], U8) for t in range(PACK)]
         y_bank = []
@@ -111,17 +109,16 @@ def tile_picked_twocdsoftbrmssend_none_p_kernel(
             )
             y_bank.append(bank)
 
+        ca_codes = pick_words("ca_codes", l_ca)
         sq_win = [sbuf("sq_win%d" % t, [P, 2 * S], F32) for t in range(PACK)]
         y_win = [sbuf("y_win%d" % t, [P, 2 * S], F32) for t in range(PACK)]
         sent = [sbuf("sent%d" % t, [P, S], F32) for t in range(PACK)]
-        denom = [sbuf("denom%d" % t, [P, S], F32) for t in range(PACK)]
+        sq_copy = [sbuf("sq_copy%d" % t, [P, S], F32) for t in range(PACK)]
         inv_root = [sbuf("inv_root%d" % t, [P, S], F32) for t in range(PACK)]
-        z = sbuf("z", [P, PACK, S], F32)
-        z2 = sbuf("z2", [P, PACK, S], F32)
 
         def square(t):
             nc.scalar.activation(sq_win[t][:, :S], y_bank[t][:], ACT.Square)
-            nc.sync.dma_start(y_win[t][:, S:], sq_win[t][:, :S])
+            nc.sync.dma_start(sq_copy[t][:], sq_win[t][:, :S])
 
         def positive_part(t):
             nc.vector.tensor_scalar(sq_win[t][:, S:], y_bank[t][:], 0.0, gain2[:, t : t + 1], ALU.max, ALU.mult)
@@ -138,10 +135,10 @@ def tile_picked_twocdsoftbrmssend_none_p_kernel(
                 nc.scalar.activation(window, src, ACT.Copy)
 
         def sum_squares(t):
-            nc.vector.tensor_tensor(denom[t][:], sq_win[t][:].indirect(l_n1[:]), y_win[t][:, S:], ALU.add)
+            nc.vector.tensor_tensor(y_win[t][:, S:], sq_win[t][:].indirect(l_n1[:]), sq_copy[t][:], ALU.add)
 
         def root(t):
-            nc.scalar.activation(inv_root[t][:], denom[t][:], ACT.Abs_reciprocal_sqrt, bias=quarter[:])
+            nc.scalar.activation(inv_root[t][:], y_win[t][:, S:], ACT.Abs_reciprocal_sqrt, bias=quarter[:])
 
         def make_z(t):
             nc.vector.tensor_tensor(z[:, t, :], y_win[t][:].indirect(l_n2[:]), inv_root[t][:], ALU.mult)
@@ -181,36 +178,48 @@ def tile_picked_twocdsoftbrmssend_none_p_kernel(
         for t in range(PACK):
             square(t)
             positive_part(t)
-        send(0, 0)
-        for t in range(1, PACK):
+        for t in range(PACK):
             send(t, 0)
+        for t in range(1, PACK):
             send(t, 1)
-        ca_codes = pick_words("ca_codes", l_ca, "w_bf")
-        cb_bytes = pick_bytes("cb_bytes", l_cb, "w_bytes0")
-        cb_codes = pick_words("cb_codes", l_cb, "w_codes0")
+        cb_codes = pick_words("cb_codes", l_cb, "w_bf")
+        cb_bytes = pick_bytes("cb_bytes", l_cb, "w_bytes3")
         for t in range(PACK):
             sum_squares(t)
         send(0, 1, on_vector=True)
+        z2 = sbuf("z2", [P, PACK, S], F32, "sq_copy3")
         for t in range(PACK):
             make_z2(t)
+        ca_bytes = pick_bytes("ca_bytes", l_ca, "sent2")
         z2_bf = weave("z2_bf", z2)
         z2_codes, z2_bytes = quantise("z2", z2_bf)
         b_bank = score("b_bank", 4, cb_codes, cb_bytes, z2_codes, z2_bytes)
+        z = sbuf("z", [P, PACK, S], F32, "sq_copy3")
         for t in range(PACK):
-            scaled_y(t)
             root(t)
+            scaled_y(t)
             make_z(t)
         z_bf = weave("z_bf", z)
+
+        minus_tanh = [sbuf("minus_tanh%d" % c, [P, S], F32) for c in range(4)]
+        product = [sbuf("product%d" % c, [P, S], F32, "sq_copy3" if c == 0 else None) for c in range(4)]
+
+        fetched_a = [None] + [sbuf("fetched_a%d" % c, [P, S], F32) for c in range(1, 4)]
+        result = [sbuf("result%d" % c, [P, S], F32) for c in range(4)]
+
         z_codes, z_bytes = quantise("z", z_bf)
         a_bank = score("a_bank", 0, ca_codes, ca_bytes, z_codes, z_bytes)
-
         for c in range(4):
-            minus_tanh = sbuf("minus_tanh%d" % c, [P, S], F32)
-            nc.scalar.activation(minus_tanh[:], b_bank[c][:], ACT.Tanh, scale=-0.0625)
+            nc.scalar.activation(minus_tanh[c][:], b_bank[c][:], ACT.Tanh, scale=-0.0625)
             nc.scalar.activation(b_win[c][:, :S], b_bank[c][:], ACT.Copy, scale=0.0625)
+        for c in range(4):
             nc.scalar.activation(a_win[c][:, :S], a_bank[c][:], ACT.Copy, scale=0.0625)
-            product = sbuf("product%d" % c, [P, S], F32)
-            nc.vector.tensor_tensor(product[:], b_win[c][:].indirect(l_n5[:]), minus_tanh[:], ALU.mult)
-            result = sbuf("result%d" % c, [P, S], F32)
-            nc.vector.tensor_tensor(result[:], a_win[c][:].indirect(l_n4[:]), product[:], ALU.add)
-            nc.sync.dma_start(out[P * c : P * (c + 1), :], result[:])
+        for c in range(1, 4):
+            nc.scalar.activation(fetched_a[c][:], a_win[c][:].indirect(l_n4[:]), ACT.Copy)
+        for c in range(4):
+            nc.vector.tensor_tensor(product[c][:], b_win[c][:].indirect(l_n5[:]), minus_tanh[c][:], ALU.mult)
+        nc.vector.tensor_tensor(result[0][:], a_win[0][:].indirect(l_n4[:]), product[0][:], ALU.add)
+        nc.sync.dma_start(out[0:P, :], result[0][:])
+        for c in range(1, 4):
+            nc.vector.tensor_tensor(result[c][:], fetched_a[c][:], product[c][:], ALU.add)
+            nc.sync.dma_start(out[P * c : P * (c + 1), :], result[c][:])

@@ -19,6 +19,7 @@ P = 128
 PACK = 4
 SPARE = 16
 HALF = S // 2
+SCALAR_SHARE = 192
 
 
 def tile_picked_twocdsoftbrmssend_none_p_kernel(
@@ -39,22 +40,19 @@ def tile_picked_twocdsoftbrmssend_none_p_kernel(
 
         table_words = sbuf("table_words", [P, T], U32)
         table_bytes = sbuf("table_bytes", [P, T], U8)
-        nc.gpsimd.memset(table_bytes[:].bitcast(I32), 0)
-        for q in range(4):
-            nc.gpsimd.dma_start(
-                table_bytes[32 * q : 32 * q + 4, :].bitcast(I32), x_scales[0, 4 * q : 4 * q + 4, :].bitcast(I32)
-            )
-
+        landed_bytes = sbuf("landed_bytes", [P, T // 4], I32)
         w_raw = [sbuf("w_raw%d" % u, [P, PACK, H // 2], F32) for u in range(2)]
         w_rows = w1.rearrange("(p j) c -> p j c", j=PACK)
-        nc.scalar.dma_start(table_words[:].bitcast(I32), x_words[0].rearrange("p n t -> p (n t)").bitcast(I32))
-        nc.scalar.dma_start(w_raw[0][:], w_rows[:, :, 0 : H // 2])
-        nc.scalar.dma_start(w_raw[1][:], w_rows[:, :, H // 2 : H])
-
         gain = sbuf("gain", [P, PACK], F32)
         gain2 = sbuf("gain2", [P, PACK], F32)
+
         l_offs = load_list("l_offs", offs)
+        for q in range(4):
+            nc.sync.dma_start(landed_bytes[32 * q : 32 * q + 4, :], x_scales[0, 4 * q : 4 * q + 4, :].bitcast(I32))
+        nc.sync.dma_start(w_raw[0][:], w_rows[:, :, 0 : H // 2])
         l_ca = load_list("l_ca", ca)
+        nc.sync.dma_start(w_raw[1][:], w_rows[:, :, H // 2 : H])
+        nc.sync.dma_start(table_words[:].bitcast(I32), x_words[0].rearrange("p n t -> p (n t)").bitcast(I32))
         l_cb = load_list("l_cb", cb)
         nc.sync.dma_start(gain2[:], gs2.rearrange("(p t) o -> p (t o)", t=PACK))
         l_n3 = load_list("l_n3", n3)
@@ -64,8 +62,11 @@ def tile_picked_twocdsoftbrmssend_none_p_kernel(
         l_n5 = load_list("l_n5", n5)
         l_n4 = load_list("l_n4", n4)
 
+        nc.vector.memset(table_bytes[:].bitcast(I32), 0)
         quarter = sbuf("quarter", [P, 1], F32)
         nc.vector.memset(quarter[:], 0.25)
+        warm = sbuf("warm", [P, 1], F32)
+        nc.scalar.activation(warm[:], quarter[:], ACT.Abs_reciprocal_sqrt, bias=quarter[:])
         a_win = [sbuf("a_win%d" % c, [P, S + SPARE], F32) for c in range(4)]
         b_win = [sbuf("b_win%d" % c, [P, S + SPARE], F32) for c in range(4)]
         for tile in a_win + b_win:
@@ -78,9 +79,9 @@ def tile_picked_twocdsoftbrmssend_none_p_kernel(
             nc.vector.tensor_copy(tile[:], table_bytes[:].indirect(offsets[:]))
             return tile
 
-        def pick_words(name, offsets, tag=None):
-            tile = sbuf(name, [P, S], U32, tag)
-            nc.vector.tensor_copy(tile[:], table_words[:].indirect(offsets[:]))
+        def pick_words(name, offsets):
+            tile = sbuf(name, [P, 16 * offsets.shape[1]], U32)
+            nc.vector.tensor_copy(tile[:], table_words[:].indirect(offsets))
             return tile
 
         w_bf = sbuf("w_bf", [P, PACK, P, PACK], BF16)
@@ -91,8 +92,10 @@ def tile_picked_twocdsoftbrmssend_none_p_kernel(
                 w_raw[u][:].rearrange("p j (m t) -> p m j t", t=PACK),
             )
 
-        x_codes = pick_words("x_codes", l_offs)
+        for q in range(4):
+            nc.vector.tensor_copy(table_bytes[32 * q : 32 * q + 4, :].bitcast(I32), landed_bytes[32 * q : 32 * q + 4, :])
         x_bytes = pick_bytes("x_bytes", l_offs)
+        x_codes = [pick_words("x_codes%d" % h, l_offs[:, 16 * h : 16 * h + 16]) for h in range(2)]
         cast_w(0)
         cast_w(1)
         w_codes = [sbuf("w_codes%d" % t, [P, P], U32) for t in range(PACK)]
@@ -103,13 +106,16 @@ def tile_picked_twocdsoftbrmssend_none_p_kernel(
                 out=w_codes[t][:].bitcast(FP8X4), scales=w_bytes[t][:], in_=w_bf[:, t].rearrange("p m j -> p (m j)")
             )
             bank = psum.tile([P, S], F32, name="y_bank%d" % t, tag="bank%d" % t)
-            nc.tensor.matmul_mx(
-                out=bank[:], lhsT=w_codes[t][:].bitcast(FP8X4), lhsT_scale=w_bytes[t][:],
-                rhs=x_codes[:].bitcast(FP8X4), rhs_scale=x_bytes[:], start=True, stop=True,
-            )
+            for h in range(2):
+                cols = slice(HALF * h, HALF * (h + 1))
+                nc.tensor.matmul_mx(
+                    out=bank[:, cols], lhsT=w_codes[t][:].bitcast(FP8X4), lhsT_scale=w_bytes[t][:],
+                    rhs=x_codes[h][:].bitcast(FP8X4), rhs_scale=x_bytes[:, cols], start=True, stop=True,
+                )
             y_bank.append(bank)
 
-        ca_codes = pick_words("ca_codes", l_ca)
+        ca_bytes = pick_bytes("ca_bytes", l_ca)
+        ca_codes = pick_words("ca_codes", l_ca[:])
         sq_win = [sbuf("sq_win%d" % t, [P, 2 * S], F32) for t in range(PACK)]
         y_win = [sbuf("y_win%d" % t, [P, 2 * S], F32) for t in range(PACK)]
         sent = [sbuf("sent%d" % t, [P, S], F32) for t in range(PACK)]
@@ -126,9 +132,9 @@ def tile_picked_twocdsoftbrmssend_none_p_kernel(
         def scaled_y(t):
             nc.scalar.activation(y_win[t][:, :S], y_bank[t][:], ACT.Copy, scale=gain[:, t : t + 1])
 
-        def send(t, half, on_vector=False):
-            window = sent[t][:].indirect(l_n3[:, 16 * half : 16 * half + 16])
-            src = sq_win[t][:, S + HALF * half : S + HALF * (half + 1)]
+        def send(t, first, last, on_vector=False):
+            window = sent[t][:].indirect(l_n3[:, first // 16 : last // 16])
+            src = sq_win[t][:, S + first : S + last]
             if on_vector:
                 nc.vector.tensor_copy(window, src)
             else:
@@ -149,57 +155,60 @@ def tile_picked_twocdsoftbrmssend_none_p_kernel(
             )
 
         def weave(name, planes):
-            tile = sbuf(name, [P, S, PACK], BF16)
+            tile = sbuf(name, [P, planes.shape[2], PACK], BF16)
             nc.vector.tensor_copy(
-                tile[:].rearrange("p (c i) t -> p c t i", i=4), planes[:].rearrange("p t (c i) -> p c t i", i=4)
+                tile[:].rearrange("p (c i) t -> p c t i", i=4), planes.rearrange("p t (c i) -> p c t i", i=4)
             )
             return tile
 
         def quantise(name, woven):
-            codes = sbuf(name + "_codes", [P, S], U32)
-            scale_bytes = sbuf(name + "_bytes", [P, S], U8)
+            codes = sbuf(name + "_codes", [P, woven.shape[1]], U32)
+            scale_bytes = sbuf(name + "_bytes", [P, woven.shape[1]], U8)
             nc.vector.quantize_mx(
                 out=codes[:].bitcast(FP8X4), scales=scale_bytes[:], in_=woven[:].rearrange("p n t -> p (n t)")
             )
             return codes, scale_bytes
 
-        def score(name, first_bank, picked_codes, picked_bytes, codes, scale_bytes):
+        def score(name, first_bank, picked_codes, picked_bytes, quantised):
             banks = []
             for c in range(4):
                 bank = psum.tile([P, S], F32, name="%s%d" % (name, c), tag="bank%d" % (first_bank + c))
-                cols = slice(P * c, P * (c + 1))
-                nc.tensor.matmul_mx(
-                    out=bank[:], lhsT=picked_codes[:, cols].bitcast(FP8X4), lhsT_scale=picked_bytes[:, cols],
-                    rhs=codes[:].bitcast(FP8X4), rhs_scale=scale_bytes[:], start=True, stop=True,
-                )
+                rows = slice(P * c, P * (c + 1))
+                width = S // len(quantised)
+                for h, (codes, scale_bytes) in enumerate(quantised):
+                    nc.tensor.matmul_mx(
+                        out=bank[:, width * h : width * (h + 1)],
+                        lhsT=picked_codes[:, rows].bitcast(FP8X4), lhsT_scale=picked_bytes[:, rows],
+                        rhs=codes[:].bitcast(FP8X4), rhs_scale=scale_bytes[:], start=True, stop=True,
+                    )
                 banks.append(bank)
             return banks
 
         for t in range(PACK):
             square(t)
             positive_part(t)
-        for t in range(PACK):
-            send(t, 0)
+        send(0, 0, SCALAR_SHARE)
         for t in range(1, PACK):
-            send(t, 1)
-        cb_codes = pick_words("cb_codes", l_cb, "w_bf")
-        cb_bytes = pick_bytes("cb_bytes", l_cb, "w_bytes3")
+            send(t, 0, HALF)
+        for t in range(1, PACK):
+            send(t, HALF, S)
+        cb_codes = pick_words("cb_codes", l_cb[:])
         for t in range(PACK):
             sum_squares(t)
-        send(0, 1, on_vector=True)
+        send(0, SCALAR_SHARE, S, on_vector=True)
         z2 = sbuf("z2", [P, PACK, S], F32, "sq_copy3")
         for t in range(PACK):
             make_z2(t)
-        ca_bytes = pick_bytes("ca_bytes", l_ca, "sent2")
-        z2_bf = weave("z2_bf", z2)
-        z2_codes, z2_bytes = quantise("z2", z2_bf)
-        b_bank = score("b_bank", 4, cb_codes, cb_bytes, z2_codes, z2_bytes)
+        cb_bytes = pick_bytes("cb_bytes", l_cb, "sent2")
+        z2_bf = weave("z2_bf", z2[:])
         z = sbuf("z", [P, PACK, S], F32, "sq_copy3")
         for t in range(PACK):
             root(t)
             scaled_y(t)
             make_z(t)
-        z_bf = weave("z_bf", z)
+            if t == 0:
+                b_bank = score("b_bank", 4, cb_codes, cb_bytes, [quantise("z2", z2_bf)])
+        z_bf = [weave("z_bf%d" % h, z[:, :, HALF * h : HALF * (h + 1)]) for h in range(2)]
 
         minus_tanh = [sbuf("minus_tanh%d" % c, [P, S], F32) for c in range(4)]
         product = [sbuf("product%d" % c, [P, S], F32, "sq_copy3" if c == 0 else None) for c in range(4)]
@@ -207,19 +216,23 @@ def tile_picked_twocdsoftbrmssend_none_p_kernel(
         fetched_a = [None] + [sbuf("fetched_a%d" % c, [P, S], F32) for c in range(1, 4)]
         result = [sbuf("result%d" % c, [P, S], F32) for c in range(4)]
 
-        z_codes, z_bytes = quantise("z", z_bf)
-        a_bank = score("a_bank", 0, ca_codes, ca_bytes, z_codes, z_bytes)
+        a_bank = score("a_bank", 0, ca_codes, ca_bytes, [quantise("z%d" % h, z_bf[h]) for h in range(2)])
         for c in range(4):
             nc.scalar.activation(minus_tanh[c][:], b_bank[c][:], ACT.Tanh, scale=-0.0625)
             nc.scalar.activation(b_win[c][:, :S], b_bank[c][:], ACT.Copy, scale=0.0625)
         for c in range(4):
             nc.scalar.activation(a_win[c][:, :S], a_bank[c][:], ACT.Copy, scale=0.0625)
-        for c in range(1, 4):
-            nc.scalar.activation(fetched_a[c][:], a_win[c][:].indirect(l_n4[:]), ACT.Copy)
+        pieces = [(1, 0, S), (2, 0, S), (3, 0, HALF), (3, HALF, S - P), (3, S - P, S)]
+        for c, first, last in pieces:
+            nc.scalar.activation(
+                fetched_a[c][:, first:last], a_win[c][:].indirect(l_n4[:, first // 16 : last // 16]), ACT.Copy
+            )
         for c in range(4):
             nc.vector.tensor_tensor(product[c][:], b_win[c][:].indirect(l_n5[:]), minus_tanh[c][:], ALU.mult)
         nc.vector.tensor_tensor(result[0][:], a_win[0][:].indirect(l_n4[:]), product[0][:], ALU.add)
         nc.sync.dma_start(out[0:P, :], result[0][:])
-        for c in range(1, 4):
-            nc.vector.tensor_tensor(result[c][:], fetched_a[c][:], product[c][:], ALU.add)
-            nc.sync.dma_start(out[P * c : P * (c + 1), :], result[c][:])
+        for c, first, last in pieces:
+            nc.vector.tensor_tensor(
+                result[c][:, first:last], fetched_a[c][:, first:last], product[c][:, first:last], ALU.add
+            )
+            nc.sync.dma_start(out[P * c : P * (c + 1), first:last], result[c][:, first:last])

@@ -19,7 +19,7 @@ P = 128
 PACK = 4
 SPARE = 16
 HALF = S // 2
-SCALAR_SHARE = 192
+SCALAR_SHARE = 160
 
 
 def tile_picked_twocdsoftbrmssend_none_p_kernel(
@@ -51,9 +51,9 @@ def tile_picked_twocdsoftbrmssend_none_p_kernel(
             nc.sync.dma_start(landed_bytes[32 * q : 32 * q + 4, :], x_scales[0, 4 * q : 4 * q + 4, :].bitcast(I32))
         nc.sync.dma_start(w_raw[0][:], w_rows[:, :, 0 : H // 2])
         l_ca = load_list("l_ca", ca)
+        l_cb = load_list("l_cb", cb)
         nc.sync.dma_start(w_raw[1][:], w_rows[:, :, H // 2 : H])
         nc.sync.dma_start(table_words[:].bitcast(I32), x_words[0].rearrange("p n t -> p (n t)").bitcast(I32))
-        l_cb = load_list("l_cb", cb)
         nc.sync.dma_start(gain2[:], gs2.rearrange("(p t) o -> p (t o)", t=PACK))
         l_n3 = load_list("l_n3", n3)
         l_n1 = load_list("l_n1", n1)
@@ -75,8 +75,8 @@ def tile_picked_twocdsoftbrmssend_none_p_kernel(
         nc.vector.tensor_scalar(minus_half_gain2[:], gain2[:], -0.5, None, ALU.mult)
 
         def pick_bytes(name, offsets, tag=None):
-            tile = sbuf(name, [P, S], U8, tag)
-            nc.vector.tensor_copy(tile[:], table_bytes[:].indirect(offsets[:]))
+            tile = sbuf(name, [P, 16 * offsets.shape[1]], U8, tag)
+            nc.vector.tensor_copy(tile[:], table_bytes[:].indirect(offsets))
             return tile
 
         def pick_words(name, offsets):
@@ -94,8 +94,10 @@ def tile_picked_twocdsoftbrmssend_none_p_kernel(
 
         for q in range(4):
             nc.vector.tensor_copy(table_bytes[32 * q : 32 * q + 4, :].bitcast(I32), landed_bytes[32 * q : 32 * q + 4, :])
-        x_bytes = pick_bytes("x_bytes", l_offs)
+        x_bytes = pick_bytes("x_bytes", l_offs[:])
         x_codes = [pick_words("x_codes%d" % h, l_offs[:, 16 * h : 16 * h + 16]) for h in range(2)]
+        ca_bytes = pick_bytes("ca_bytes", l_ca[:])
+        cb_bytes = [pick_bytes("cb_bytes0", l_cb[:, 0:16])]
         cast_w(0)
         cast_w(1)
         w_codes = [sbuf("w_codes%d" % t, [P, P], U32) for t in range(PACK)]
@@ -114,13 +116,11 @@ def tile_picked_twocdsoftbrmssend_none_p_kernel(
                 )
             y_bank.append(bank)
 
-        ca_bytes = pick_bytes("ca_bytes", l_ca)
         ca_codes = pick_words("ca_codes", l_ca[:])
         sq_win = [sbuf("sq_win%d" % t, [P, 2 * S], F32) for t in range(PACK)]
         y_win = [sbuf("y_win%d" % t, [P, 2 * S], F32) for t in range(PACK)]
         sent = [sbuf("sent%d" % t, [P, S], F32) for t in range(PACK)]
         sq_copy = [sbuf("sq_copy%d" % t, [P, S], F32) for t in range(PACK)]
-        inv_root = [sbuf("inv_root%d" % t, [P, S], F32) for t in range(PACK)]
 
         def square(t):
             nc.scalar.activation(sq_win[t][:, :S], y_bank[t][:], ACT.Square)
@@ -178,7 +178,7 @@ def tile_picked_twocdsoftbrmssend_none_p_kernel(
                 for h, (codes, scale_bytes) in enumerate(quantised):
                     nc.tensor.matmul_mx(
                         out=bank[:, width * h : width * (h + 1)],
-                        lhsT=picked_codes[:, rows].bitcast(FP8X4), lhsT_scale=picked_bytes[:, rows],
+                        lhsT=picked_codes[:, rows].bitcast(FP8X4), lhsT_scale=picked_bytes[c],
                         rhs=codes[:].bitcast(FP8X4), rhs_scale=scale_bytes[:], start=True, stop=True,
                     )
                 banks.append(bank)
@@ -199,15 +199,17 @@ def tile_picked_twocdsoftbrmssend_none_p_kernel(
         z2 = sbuf("z2", [P, PACK, S], F32, "sq_copy3")
         for t in range(PACK):
             make_z2(t)
-        cb_bytes = pick_bytes("cb_bytes", l_cb, "sent2")
+            if t == 1:
+                cb_bytes.append(pick_bytes("cb_bytes1", l_cb[:, 16:32], "sent1"))
         z2_bf = weave("z2_bf", z2[:])
         z = sbuf("z", [P, PACK, S], F32, "sq_copy3")
+        inv_root = [sbuf("inv_root%d" % t, [P, S], F32, "sq_win%d" % (PACK - 1 - t)) for t in range(PACK)]
         for t in range(PACK):
             root(t)
             scaled_y(t)
             make_z(t)
             if t == 0:
-                b_bank = score("b_bank", 4, cb_codes, cb_bytes, [quantise("z2", z2_bf)])
+                b_bank = score("b_bank", 4, cb_codes, [cb_bytes[c // 2][:, P * (c % 2) : P * (c % 2 + 1)] for c in range(4)], [quantise("z2", z2_bf)])
         z_bf = [weave("z_bf%d" % h, z[:, :, HALF * h : HALF * (h + 1)]) for h in range(2)]
 
         minus_tanh = [sbuf("minus_tanh%d" % c, [P, S], F32) for c in range(4)]
@@ -216,7 +218,7 @@ def tile_picked_twocdsoftbrmssend_none_p_kernel(
         fetched_a = [None] + [sbuf("fetched_a%d" % c, [P, S], F32) for c in range(1, 4)]
         result = [sbuf("result%d" % c, [P, S], F32) for c in range(4)]
 
-        a_bank = score("a_bank", 0, ca_codes, ca_bytes, [quantise("z%d" % h, z_bf[h]) for h in range(2)])
+        a_bank = score("a_bank", 0, ca_codes, [ca_bytes[:, P * c : P * (c + 1)] for c in range(4)], [quantise("z%d" % h, z_bf[h]) for h in range(2)])
         for c in range(4):
             nc.scalar.activation(minus_tanh[c][:], b_bank[c][:], ACT.Tanh, scale=-0.0625)
             nc.scalar.activation(b_win[c][:, :S], b_bank[c][:], ACT.Copy, scale=0.0625)

from contextlib import ExitStack

import concourse.mybir as mybir

K, T, S, H, C = 512, 2048, 512, 512, 512
FLOPS = 3 * 2 * 512 * 512 * 512

F32 = mybir.dt.float32
BF16 = mybir.dt.bfloat16
I32 = mybir.dt.int32
U32 = mybir.dt.uint32
U16 = mybir.dt.uint16
U8 = mybir.dt.uint8
FP8X4 = mybir.dt.float8_e4m3fn_x4
ACT = mybir.ActivationFunctionType
ALU = mybir.AluOpType

P = 128
PACK = 4
SPARE = 16
HALF = S // 2
SCALAR_SHARE = 160


def tile_picked_twocdsoftbrmssend_none_p_kernel(
    tc, x_words, x_scales, w1, gs, gs2, offs, n1, n2, n3, ca, cb, n4, n5, out
):
    nc = tc.nc
    with ExitStack() as ctx:
        keep = ctx.enter_context(tc.tile_pool(name="keep", bufs=1))
        psum = ctx.enter_context(tc.psum_pool(name="psum", bufs=1))

        def sbuf(name, shape, dtype, tag=None):
            return keep.tile(shape, dtype, name=name, tag=tag or name, align_bytes=64)

        def load_list(name, src):
            tile = keep.tile([P, S // 16], U16, name=name)
            nc.sync.dma_start(tile[:], src)
            return tile

        table_words = sbuf("table_words", [P, T], U32)
        table_bytes = sbuf("table_bytes", [P, T], U8)
        landed_bytes = sbuf("landed_bytes", [P, T // 4], I32)
        w_raw = [sbuf("w_raw%d" % u, [P, PACK, H // 2], F32) for u in range(2)]
        w_rows = w1.rearrange("(p j) c -> p j c", j=PACK)
        gain = sbuf("gain", [P, PACK], F32)
        gain2 = sbuf("gain2", [P, PACK], F32)

        l_offs = load_list("l_offs", offs)
        for q in range(4):
            nc.sync.dma_start(landed_bytes[32 * q : 32 * q + 4, :], x_scales[0, 4 * q : 4 * q + 4, :].bitcast(I32))
        nc.sync.dma_start(w_raw[0][:], w_rows[:, :, 0 : H // 2])
        l_ca = load_list("l_ca", ca)
        l_cb = load_list("l_cb", cb)
        nc.sync.dma_start(w_raw[1][:], w_rows[:, :, H // 2 : H])
        nc.sync.dma_start(table_words[:].bitcast(I32), x_words[0].rearrange("p n t -> p (n t)").bitcast(I32))
        nc.sync.dma_start(gain2[:], gs2.rearrange("(p t) o -> p (t o)", t=PACK))
        l_n3 = load_list("l_n3", n3)
        l_n1 = load_list("l_n1", n1)
        nc.sync.dma_start(gain[:], gs.rearrange("(p t) o -> p (t o)", t=PACK))
        l_n2 = load_list("l_n2", n2)
        l_n5 = load_list("l_n5", n5)
        l_n4 = load_list("l_n4", n4)

        nc.vector.memset(table_bytes[:].bitcast(I32), 0)
        quarter = sbuf("quarter", [P, 1], F32)
        nc.vector.memset(quarter[:], 0.25)
        warm = sbuf("warm", [P, 1], F32)
        nc.scalar.activation(warm[:], quarter[:], ACT.Abs_reciprocal_sqrt, bias=quarter[:])
        a_win = [sbuf("a_win%d" % c, [P, S + SPARE], F32) for c in range(4)]
        b_win = [sbuf("b_win%d" % c, [P, S + SPARE], F32) for c in range(4)]
        for tile in a_win + b_win:
            nc.vector.memset(tile[:, S:], 0.0)
        minus_half_gain2 = sbuf("minus_half_gain2", [P, PACK], F32)
        nc.vector.tensor_scalar(minus_half_gain2[:], gain2[:], -0.5, None, ALU.mult)

        def pick_bytes(name, offsets, tag=None):
            tile = sbuf(name, [P, 16 * offsets.shape[1]], U8, tag)
            nc.vector.tensor_copy(tile[:], table_bytes[:].indirect(offsets))
            return tile

        def pick_words(name, offsets):
            tile = sbuf(name, [P, 16 * offsets.shape[1]], U32)
            nc.vector.tensor_copy(tile[:], table_words[:].indirect(offsets))
            return tile

        w_bf = sbuf("w_bf", [P, PACK, P, PACK], BF16)

        def cast_w(u):
            nc.scalar.copy(
                w_bf[:, :, 64 * u : 64 * u + 64, :].rearrange("p t m j -> p m j t"),
                w_raw[u][:].rearrange("p j (m t) -> p m j t", t=PACK),
            )

        for q in range(4):
            nc.vector.tensor_copy(table_bytes[32 * q : 32 * q + 4, :].bitcast(I32), landed_bytes[32 * q : 32 * q + 4, :])
        x_bytes = pick_bytes("x_bytes", l_offs[:])
        x_codes = [pick_words("x_codes%d" % h, l_offs[:, 16 * h : 16 * h + 16]) for h in range(2)]
        ca_bytes = pick_bytes("ca_bytes", l_ca[:])
        cb_bytes = [pick_bytes("cb_bytes0", l_cb[:, 0:16])]
        cast_w(0)
        cast_w(1)
        w_codes = [sbuf("w_codes%d" % t, [P, P], U32) for t in range(PACK)]
        w_bytes = [sbuf("w_bytes%d" % t, [P, P], U8) for t in range(PACK)]
        y_bank = []
        for t in range(PACK):
            nc.vector.quantize_mx(
                out=w_codes[t][:].bitcast(FP8X4), scales=w_bytes[t][:], in_=w_bf[:, t].rearrange("p m j -> p (m j)")
            )
            bank = psum.tile([P, S], F32, name="y_bank%d" % t, tag="bank%d" % t)
            for h in range(2):
                cols = slice(HALF * h, HALF * (h + 1))
                nc.tensor.matmul_mx(
                    out=bank[:, cols], lhsT=w_codes[t][:].bitcast(FP8X4), lhsT_scale=w_bytes[t][:],
                    rhs=x_codes[h][:].bitcast(FP8X4), rhs_scale=x_bytes[:, cols], start=True, stop=True,
                )
            y_bank.append(bank)

        ca_codes = pick_words("ca_codes", l_ca[:])
        sq_win = [sbuf("sq_win%d" % t, [P, 2 * S], F32) for t in range(PACK)]
        y_win = [sbuf("y_win%d" % t, [P, 2 * S], F32) for t in range(PACK)]
        sent = [sbuf("sent%d" % t, [P, S], F32) for t in range(PACK)]
        sq_copy = [sbuf("sq_copy%d" % t, [P, S], F32) for t in range(PACK)]

        def square(t):
            nc.scalar.activation(sq_win[t][:, :S], y_bank[t][:], ACT.Square)
            nc.sync.dma_start(sq_copy[t][:], sq_win[t][:, :S])

        def positive_part(t):
            nc.vector.tensor_scalar(sq_win[t][:, S:], y_bank[t][:], 0.0, gain2[:, t : t + 1], ALU.max, ALU.mult)

        def scaled_y(t):
            nc.scalar.activation(y_win[t][:, :S], y_bank[t][:], ACT.Copy, scale=gain[:, t : t + 1])

        def send(t, first, last, on_vector=False):
            window = sent[t][:].indirect(l_n3[:, first // 16 : last // 16])
            src = sq_win[t][:, S + first : S + last]
            if on_vector:
                nc.vector.tensor_copy(window, src)
            else:
                nc.scalar.activation(window, src, ACT.Copy)

        def sum_squares(t):
            nc.vector.tensor_tensor(y_win[t][:, S:], sq_win[t][:].indirect(l_n1[:]), sq_copy[t][:], ALU.add)

        def root(t):
            nc.scalar.activation(inv_root[t][:], y_win[t][:, S:], ACT.Abs_reciprocal_sqrt, bias=quarter[:])

        def make_z(t):
            nc.vector.tensor_tensor(z[:, t, :], y_win[t][:].indirect(l_n2[:]), inv_root[t][:], ALU.mult)

        def make_z2(t):
            nc.vector.scalar_tensor_tensor(
                z2[:, t, :], y_bank[t][:], minus_half_gain2[:, t : t + 1], sent[t][:], ALU.mult, ALU.add
            )

        def weave(name, planes):
            tile = sbuf(name, [P, planes.shape[2], PACK], BF16)
            nc.vector.tensor_copy(
                tile[:].rearrange("p (c i) t -> p c t i", i=4), planes.rearrange("p t (c i) -> p c t i", i=4)
            )
            return tile

        def quantise(name, woven):
            codes = sbuf(name + "_codes", [P, woven.shape[1]], U32)
            scale_bytes = sbuf(name + "_bytes", [P, woven.shape[1]], U8)
            nc.vector.quantize_mx(
                out=codes[:].bitcast(FP8X4), scales=scale_bytes[:], in_=woven[:].rearrange("p n t -> p (n t)")
            )
            return codes, scale_bytes

        def score(name, first_bank, picked_codes, picked_bytes, quantised):
            banks = []
            for c in range(4):
                bank = psum.tile([P, S], F32, name="%s%d" % (name, c), tag="bank%d" % (first_bank + c))
                rows = slice(P * c, P * (c + 1))
                width = S // len(quantised)
                for h, (codes, scale_bytes) in enumerate(quantised):
                    nc.tensor.matmul_mx(
                        out=bank[:, width * h : width * (h + 1)],
                        lhsT=picked_codes[:, rows].bitcast(FP8X4), lhsT_scale=picked_bytes[c],
                        rhs=codes[:].bitcast(FP8X4), rhs_scale=scale_bytes[:], start=True, stop=True,
                    )
                banks.append(bank)
            return banks

        for t in range(PACK):
            square(t)
            positive_part(t)
        send(0, 0, SCALAR_SHARE)
        for t in range(1, PACK):
            send(t, 0, HALF)
        for t in range(1, PACK):
            send(t, HALF, S)
        cb_codes = pick_words("cb_codes", l_cb[:])
        for t in range(PACK):
            sum_squares(t)
        send(0, SCALAR_SHARE, S, on_vector=True)
        z2 = sbuf("z2", [P, PACK, S], F32, "sq_copy3")
        for t in range(PACK):
            make_z2(t)
            if t == 1:
                cb_bytes.append(pick_bytes("cb_bytes1", l_cb[:, 16:32], "sent1"))
        z2_bf = weave("z2_bf", z2[:])
        z = sbuf("z", [P, PACK, S], F32, "sq_copy3")
        inv_root = [sbuf("inv_root%d" % t, [P, S], F32, "sq_win%d" % (PACK - 1 - t)) for t in range(PACK)]
        for t in range(PACK):
            root(t)
            scaled_y(t)
            make_z(t)
            if t == 0:
                b_bank = score("b_bank", 4, cb_codes, [cb_bytes[c // 2][:, P * (c % 2) : P * (c % 2 + 1)] for c in range(4)], [quantise("z2", z2_bf)])
        z_bf = [weave("z_bf%d" % h, z[:, :, HALF * h : HALF * (h + 1)]) for h in range(2)]

        minus_tanh = [sbuf("minus_tanh%d" % c, [P, S], F32) for c in range(4)]
        product = [sbuf("product%d" % c, [P, S], F32, "sq_copy3" if c == 0 else None) for c in range(4)]

        fetched_a = [None] + [sbuf("fetched_a%d" % c, [P, S], F32) for c in range(1, 4)]
        result = [sbuf("result%d" % c, [P, S], F32) for c in range(4)]

        a_bank = score("a_bank", 0, ca_codes, [ca_bytes[:, P * c : P * (c + 1)] for c in range(4)], [quantise("z%d" % h, z_bf[h]) for h in range(2)])
        for c in range(4):
            nc.scalar.activation(minus_tanh[c][:], b_bank[c][:], ACT.Tanh, scale=-0.0625)
            nc.scalar.activation(b_win[c][:, :S], b_bank[c][:], ACT.Copy, scale=0.0625)
        for c in range(4):
            nc.scalar.activation(a_win[c][:, :S], a_bank[c][:], ACT.Copy, scale=0.0625)
        pieces = [(1, 0, S), (2, 0, S), (3, 0, HALF), (3, HALF, S - P), (3, S - P, S)]
        for c, first, last in pieces:
            nc.scalar.activation(
                fetched_a[c][:, first:last], a_win[c][:].indirect(l_n4[:, first // 16 : last // 16]), ACT.Copy
            )
        for c in range(4):
            nc.vector.tensor_tensor(product[c][:], b_win[c][:].indirect(l_n5[:]), minus_tanh[c][:], ALU.mult)
        nc.vector.tensor_tensor(result[0][:], a_win[0][:].indirect(l_n4[:]), product[0][:], ALU.add)
        nc.sync.dma_start(out[0:P, :], result[0][:])
        for c, first, last in pieces:
            nc.vector.tensor_tensor(
                result[c][:, first:last], fetched_a[c][:, first:last], product[c][:, first:last], ALU.add
            )
            nc.sync.dma_start(out[P * c : P * (c + 1), first:last], result[c][:, first:last])
